import numpy as np
import ml_dtypes


def mxq(x, axis, fmt="e4m3"):
    dtype, down = {"e4m3": (ml_dtypes.float8_e4m3fn, 7), "e5m2": (ml_dtypes.float8_e5m2, 14)}[fmt]
    v = np.moveaxis(np.asarray(x, np.float32).astype(ml_dtypes.bfloat16).astype(np.float64), axis, -1)
    blocks = v.reshape(v.shape[:-1] + (-1, 32))
    amax = np.abs(blocks).max(-1, keepdims=True)
    byte = np.maximum(np.where(amax > 0, np.frexp(amax)[1] - 1 + 127, 0) - down, 1)
    scale = np.exp2(byte - 127.0)
    codes = (blocks / scale).astype(np.float32).astype(dtype).astype(np.float64)
    return np.moveaxis((codes * scale).reshape(v.shape), -1, axis)


WIDE = False


def mx_kscale(k):
    if not WIDE:
        return np.ones(k)
    levels = np.array([10, -10, 5, -5, 0])
    if k % 512:
        return np.exp2(np.random.permutation(np.resize(levels, k // 32))).repeat(32)
    a = np.empty((k // 512, 16))
    for p in range(k // 512):
        a[p, :8] = np.random.permutation(np.resize(levels, 8))
        for g in range(8):
            far = levels[np.abs(levels - a[p, g]) >= 10]
            a[p, g + 8] = far[np.random.randint(len(far))]
    return np.exp2(a.ravel()).repeat(32)


def f64(x):
    return np.asarray(x).astype(np.float64)


def striped(idx):
    return np.tile(idx.reshape(-1, 16).T, (8, 1)).astype(np.uint16)


def unstriped(offs):
    return offs[:16].T.reshape(-1).astype(np.int64)


def pack_weight(w):
    k, n = w.shape
    w = f64(np.asarray(w, np.float32).astype(ml_dtypes.bfloat16)).reshape(k // 32, 32, n)
    amax = np.abs(w).max(1)
    byte = np.clip(np.where(amax > 0, np.frexp(amax)[1] - 1 + 127 - 7, 1), 1, 254)
    scaled = (w * np.exp2(127.0 - byte)[:, None, :]).reshape(k, n).astype(np.float32)
    words = np.ascontiguousarray(scaled.reshape(k // 512, 128, 4, n).transpose(0, 1, 3, 2)).astype(ml_dtypes.float8_e4m3fn).view(np.uint8)
    return words, np.ascontiguousarray(byte.astype(np.uint8).reshape(k // 512, 16, n))


def unpack_weight(words, scales):
    g, p, n, _ = words.shape
    vals = np.ascontiguousarray(words).view(ml_dtypes.float8_e4m3fn).astype(np.float64) * np.repeat(np.exp2(scales.astype(np.float64) - 127.0), 8, axis=1)[..., None]
    return vals.transpose(0, 1, 3, 2).reshape(g * 512, n)


K, T, S, N, H, U = 1024, 1024, 512, 128, 512, 1024


def setup_inputs():
    n = np.random.standard_normal
    s = mx_kscale(K)[:, None]
    u = mx_kscale(H)
    packed_xT = pack_weight(n((K, T)) * s)
    return {
        "x_words": packed_xT[0],
        "x_scales": packed_xT[1],
        "w1": (n((K, H)) / np.sqrt(K) / s).astype(np.float32),
        "w2": (n((K, H)) / np.sqrt(K) / s).astype(np.float32),
        "unit": (np.random.uniform(0.6, 1.4, (H, 1)) * u[:, None]).astype(np.float32),
        "w3": (n((H, N)) / np.sqrt(H) / u[:, None]).astype(np.float32),
        "offs": striped(np.random.permutation(T)[:S]),
        "pk": striped(np.random.permutation(np.concatenate([np.arange(S), np.random.randint(0, S, U - S)]))),
        "dp1": striped(np.random.permutation(np.concatenate([np.arange(S), np.random.randint(0, S, U - S)]))),
        "dp2": striped(np.random.permutation(np.concatenate([np.arange(S), np.random.randint(0, S, U - S)]))),
    }


def reference(x_words, x_scales, w1, w2, unit, w3, offs, pk, dp1, dp2):
    xq = unpack_weight(x_words, x_scales)[:, unstriped(offs)]
    y = mxq(f64(w1), 0, "e4m3").T @ xq
    yp = y[:, unstriped(pk)]
    y_1 = y[:, unstriped(dp1)]
    y_2 = y[:, unstriped(dp2)]
    cmp1 = np.minimum(yp, y_1) + y_2
    z1 = mxq(f64(w2), 0, "e4m3").T @ xq
    zp = z1[:, unstriped(pk)]
    zd2 = z1[:, unstriped(dp2)]
    hid = f64(unit) * (cmp1 * zp - zd2)
    return mxq(f64(w3), 0, "e4m3").T @ mxq(hid, 0, "e4m3")

@@ -1,0 +1,278 @@
+from contextlib import ExitStack
+
+import concourse.mybir as mybir
+
+K, T, S, N, H, U = 1024, 1024, 512, 128, 512, 1024
+FLOPS = 2 * (2 * K * H * S + H * N * U)
+
+F32 = mybir.dt.float32
+BF16 = mybir.dt.bfloat16
+I32 = mybir.dt.int32
+U32 = mybir.dt.uint32
+U16 = mybir.dt.uint16
+U8 = mybir.dt.uint8
+FP8X4 = mybir.dt.float8_e4m3fn_x4
+ALU = mybir.AluOpType
+COPY = mybir.ActivationFunctionType.Copy
+
+P = 128
+PACK = 4
+K_PASS = P * PACK
+PASSES = K // K_PASS
+LIST_ROWS = 16
+BLOCK = 512
+BLOCKS = U // BLOCK
+WINDOW = S + LIST_ROWS
+LAST_PIECES = (256, 128, 128)
+
+
+def tile_picked_yresolv_dep_p_kernel(
+    tc, x_words, x_scales, w1, w2, unit, w3, offs, pk, dp1, dp2, out
+):
+    nc = tc.nc
+    with ExitStack() as ctx:
+        keep = ctx.enter_context(tc.tile_pool(name="keep", bufs=1))
+        psum = ctx.enter_context(tc.psum_pool(name="psum", bufs=1))
+
+        def sb(name, shape, dtype):
+            return keep.tile(shape, dtype, name=name, align_bytes=64)
+
+        x_scale_rows = sb("x_scale_rows", [P, T], U8)
+        nc.vector.memset(x_scale_rows[:].bitcast(I32), 0)
+        neg_y = [sb("neg_y%d" % t, [P, WINDOW], F32) for t in range(PACK)]
+        neg_uz = [sb("neg_uz%d" % t, [P, WINDOW], F32) for t in range(PACK)]
+        for table in neg_y + neg_uz:
+            nc.gpsimd.memset(table[:, S:WINDOW], 0.0)
+
+        lists = {}
+        for name, src in (("offs", offs), ("pk", pk), ("dp1", dp1), ("dp2", dp2)):
+            lists[name] = keep.tile([P, src.shape[1]], U16, name="list_" + name)
+            nc.sync.dma_start(lists[name][:], src)
+
+        for q in range(4):
+            nc.scalar.dma_start(
+                out=x_scale_rows[32 * q : 32 * q + 4 * PASSES, :].bitcast(I32),
+                in_=x_scales[:, 4 * q : 4 * q + 4, :].bitcast(I32),
+            )
+        x_all = []
+        for g in range(PASSES):
+            words = sb("x_all%d" % g, [P, T], I32)
+            nc.sync.dma_start(out=words[:], in_=x_words[g].rearrange("p n j -> p (n j)").bitcast(I32))
+            x_all.append(words)
+        raw = {}
+        for name, w in (("w1", w1), ("w2", w2)):
+            for g in range(PASSES):
+                raw[name, g] = sb("raw_%s_%d" % (name, g), [P, PACK, H], F32)
+                nc.sync.dma_start(
+                    out=raw[name, g][:],
+                    in_=w[g * K_PASS : (g + 1) * K_PASS, :].rearrange("(p j) c -> p j c", j=PACK),
+                )
+        unit_raw = sb("unit_raw", [P, PACK, 8], F32)
+        unit_by_tile = unit.rearrange("(a t i) o -> t a i o", t=PACK, i=4)
+        with nc.allow_non_contiguous_dma(reason="one value a partition"):
+            for t in range(PACK):
+                nc.sync.dma_start(out=unit_raw[:, t, 0:1], in_=unit_by_tile[t])
+        w3_raw = sb("w3_raw", [P, PACK, N], F32)
+        w3_by_tile = w3.rearrange("(a t i) n -> t a i n", t=PACK, i=4)
+        for t in range(PACK):
+            nc.sync.dma_start(out=w3_raw[:, t, :], in_=w3_by_tile[t])
+
+        x_picked = []
+        for g in range(PASSES):
+            picked = sb("x_picked%d" % g, [P, S], U32)
+            nc.vector.tensor_copy(picked[:], x_all[g][:].bitcast(U32).indirect(lists["offs"][:]))
+            x_picked.append(picked)
+        x_picked_scales = sb("x_picked_scales", [P, S], U8)
+        nc.vector.tensor_copy(x_picked_scales[:], x_scale_rows[:].indirect(lists["offs"][:]))
+
+        grouped = {}
+        lhs = {}
+
+        def group(name, g, t0, t1, copy):
+            tile = sb("grp_%s_%d_%d" % (name, g, t0), [P, (t1 - t0) * K_PASS], BF16)
+            copy(
+                tile[:].rearrange("p (t a i j) -> p t a j i", a=32, i=4, j=PACK),
+                raw[name, g][:].rearrange("p j (a t i) -> p t a j i", t=PACK, i=4)[:, t0:t1],
+            )
+            grouped[name, g, t0] = (tile, t1)
+
+        def quantize(name, g, t0):
+            tile, t1 = grouped[name, g, t0]
+            width = (t1 - t0) * P
+            codes = sb("codes_%s_%d_%d" % (name, g, t0), [P, width], U32)
+            scales = sb("scales_%s_%d_%d" % (name, g, t0), [P, width], U8)
+            nc.vector.quantize_mx(out=codes[:].bitcast(FP8X4), scales=scales[:], in_=tile[:])
+            for t in range(t0, t1):
+                cols = slice((t - t0) * P, (t - t0 + 1) * P)
+                lhs[name, g, t] = (codes[:, cols], scales[:, cols])
+
+        acc = {}
+
+        def project(name, t):
+            acc[name, t] = psum.tile([P, S], F32, name="acc_%s_%d" % (name, t), tag="bank_%s_%d" % (name, t))
+            for g in range(PASSES):
+                codes, scales = lhs[name, g, t]
+                nc.tensor.matmul_mx(
+                    out=acc[name, t][:],
+                    lhsT=codes.bitcast(FP8X4),
+                    lhsT_scale=scales,
+                    rhs=x_picked[g][:].bitcast(FP8X4),
+                    rhs_scale=x_picked_scales[4 * g : P, :],
+                    start=(g == 0),
+                    stop=(g == PASSES - 1),
+                )
+
+        group("w1", 0, 0, 2, nc.scalar.copy)
+        group("w1", 0, 2, 4, nc.vector.tensor_copy)
+        quantize("w1", 0, 0)
+        quantize("w1", 0, 2)
+        group("w1", 1, 0, 1, nc.vector.tensor_copy)
+        group("w1", 1, 1, 3, nc.scalar.copy)
+        group("w1", 1, 3, 4, nc.vector.tensor_copy)
+        quantize("w1", 1, 0)
+        quantize("w1", 1, 3)
+        quantize("w1", 1, 1)
+        for t in range(PACK):
+            project("w1", t)
+
+        def offsets(name, c0, c1):
+            return lists[name][:, c0 // LIST_ROWS : c1 // LIST_ROWS]
+
+        steps = [(b, t) for b in range(BLOCKS) for t in range(PACK)]
+        wide = {}
+        for b in range(BLOCKS):
+            for name in ("yp", "y1", "low", "cmp"):
+                for t in range(PACK):
+                    wide[name, b, t] = sb("%s_%d_%d" % (name, b, t), [P, BLOCK], F32)
+            wide["prod", b] = sb("prod_%d" % b, [P, PACK, BLOCK], F32)
+
+        def fetch_y(s):
+            b, t = steps[s]
+            c0, c1 = b * BLOCK, (b + 1) * BLOCK
+            if b == 0:
+                nc.scalar.activation(neg_y[t][:, 0:S], acc["w1", t][:], COPY, scale=-1.0)
+            nc.scalar.activation(wide["yp", b, t][:], neg_y[t][:].indirect(offsets("pk", c0, c1)), COPY)
+            if s == 0:
+                nc.vector.tensor_copy(wide["y1", b, t][:], neg_y[t][:].indirect(offsets("dp1", c0, c1)))
+            else:
+                nc.scalar.activation(wide["y1", b, t][:], neg_y[t][:].indirect(offsets("dp1", c0, c1)), COPY)
+
+        def lower(s):
+            b, t = steps[s]
+            nc.vector.tensor_tensor(wide["low", b, t][:], wide["yp", b, t][:], wide["y1", b, t][:], ALU.max)
+
+        def add_y2(s):
+            b, t = steps[s]
+            window = neg_y[t][:].indirect(offsets("dp2", b * BLOCK, (b + 1) * BLOCK))
+            nc.vector.tensor_tensor(wide["cmp", b, t][:], window, wide["low", b, t][:], ALU.add)
+
+        def times_zp(s):
+            b, t = steps[s]
+            window = neg_uz[t][:].indirect(offsets("pk", b * BLOCK, (b + 1) * BLOCK))
+            nc.vector.tensor_tensor(wide["prod", b][:, t, :], window, wide["cmp", b, t][:], ALU.mult)
+
+        def evacuate_z(t):
+            nc.scalar.activation(neg_uz[t][:, 0:S], acc["w2", t][:], COPY, scale=neg_unit[:, t : t + 1])
+
+        zd2 = {}
+        hid = {}
+
+        def fetch_zd2(c0, c1, t):
+            if t == 0:
+                zd2[c0] = sb("zd2_%d" % c0, [P, PACK, c1 - c0], F32)
+            nc.scalar.activation(zd2[c0][:, t, :], neg_uz[t][:].indirect(offsets("dp2", c0, c1)), COPY)
+
+        def finish_hid(c0, c1):
+            b = c0 // BLOCK
+            hid[c0] = sb("hid_%d" % c0, [P, PACK * (c1 - c0)], BF16)
+            prod = wide["prod", b][:, :, c0 - b * BLOCK : c1 - b * BLOCK]
+            nc.vector.tensor_tensor(
+                hid[c0][:].rearrange("p (c i t) -> p c t i", i=4, t=PACK),
+                prod.rearrange("p t (c i) -> p c t i", i=4),
+                zd2[c0][:].rearrange("p t (c i) -> p c t i", i=4),
+                ALU.add,
+            )
+
+        def build(c0, c1, bank):
+            width = c1 - c0
+            codes = sb("hid_codes_%d" % c0, [P, width], U32)
+            scales = sb("hid_scales_%d" % c0, [P, width], U8)
+            nc.vector.quantize_mx(out=codes[:].bitcast(FP8X4), scales=scales[:], in_=hid[c0][:])
+            sums = psum.tile([P, width], F32, name="sums_%d" % c0, tag="bank_w1_%d" % bank)
+            nc.tensor.matmul_mx(
+                out=sums[:],
+                lhsT=w3_codes[:].bitcast(FP8X4),
+                lhsT_scale=w3_scales[:],
+                rhs=codes[:].bitcast(FP8X4),
+                rhs_scale=scales[:],
+                start=True,
+                stop=True,
+            )
+            result = sb("result_%d" % c0, [P, width], F32)
+            nc.scalar.copy(result[:], sums[:])
+            nc.sync.dma_start(out=out[:, c0:c1], in_=result[:])
+
+        fetch_y(0)
+        group("w2", 0, 0, 4, nc.vector.tensor_copy)
+        lower(0)
+        quantize("w2", 0, 0)
+        add_y2(0)
+        fetch_y(1)
+        group("w2", 1, 0, 2, nc.vector.tensor_copy)
+        group("w2", 1, 2, 4, nc.vector.tensor_copy)
+        quantize("w2", 1, 0)
+        neg_unit = sb("neg_unit", [P, PACK], F32)
+        nc.vector.tensor_scalar(neg_unit[:], unit_raw[:, :, 0], -1.0, None, ALU.mult)
+        quantize("w2", 1, 2)
+        for t in range(PACK):
+            project("w2", t)
+        lower(1)
+        w3_grouped = sb("w3_grouped", [P, PACK * N], BF16)
+        nc.vector.tensor_copy(
+            w3_grouped[:].rearrange("p (c i t) -> p c t i", i=4, t=PACK),
+            w3_raw[:].rearrange("p t (c i) -> p c t i", i=4),
+        )
+        add_y2(1)
+        w3_codes = sb("w3_codes", [P, N], U32)
+        w3_scales = sb("w3_scales", [P, N], U8)
+        nc.vector.quantize_mx(out=w3_codes[:].bitcast(FP8X4), scales=w3_scales[:], in_=w3_grouped[:])
+
+        fetch_y(2)
+        evacuate_z(0)
+        evacuate_z(1)
+        lower(2)
+        times_zp(0)
+        add_y2(2)
+        fetch_y(3)
+        evacuate_z(2)
+        evacuate_z(3)
+        times_zp(1)
+        lower(3)
+        times_zp(2)
+        add_y2(3)
+        for s in range(PACK, 2 * PACK):
+            fetch_y(s)
+            if s < PACK + 2:
+                fetch_zd2(0, BLOCK, 2 * (s - PACK))
+                fetch_zd2(0, BLOCK, 2 * (s - PACK) + 1)
+            lower(s)
+            times_zp(s - 1)
+            add_y2(s)
+            if s == PACK + 1:
+                finish_hid(0, BLOCK)
+            if s == PACK + 2:
+                build(0, BLOCK, 0)
+        times_zp(2 * PACK - 1)
+        c0 = BLOCK
+        pieces = []
+        for width in LAST_PIECES:
+            pieces.append((c0, c0 + width))
+            c0 = c0 + width
+        for c0, c1 in pieces:
+            for t in range(PACK):
+                fetch_zd2(c0, c1, t)
+        for n, (c0, c1) in enumerate(pieces):
+            finish_hid(c0, c1)
+            if n > 0:
+                build(pieces[n - 1][0], pieces[n - 1][1], n)
+        build(pieces[-1][0], pieces[-1][1], 0)

@@ -23,7 +23,8 @@ LIST_ROWS = 16
 BLOCK = 512
 BLOCKS = U // BLOCK
 WINDOW = S + LIST_ROWS
-LAST_PIECES = (256, 128, 128)
+FETCH_BUFS = 4
+PIECES = (512, 256, 128, 128)
 
 
 def tile_picked_yresolv_dep_p_kernel(
@@ -34,23 +35,26 @@ def tile_picked_yresolv_dep_p_kernel(
         keep = ctx.enter_context(tc.tile_pool(name="keep", bufs=1))
         psum = ctx.enter_context(tc.psum_pool(name="psum", bufs=1))
 
-        def sb(name, shape, dtype):
-            return keep.tile(shape, dtype, name=name, align_bytes=64)
+        def sb(name, shape, dtype, tag=None, bufs=1):
+            return keep.tile(shape, dtype, name=name, tag=tag or name, bufs=bufs, align_bytes=64)
 
         x_scale_rows = sb("x_scale_rows", [P, T], U8)
-        nc.vector.memset(x_scale_rows[:].bitcast(I32), 0)
+        nc.gpsimd.memset(x_scale_rows[:].bitcast(I32), 0)
         neg_y = [sb("neg_y%d" % t, [P, WINDOW], F32) for t in range(PACK)]
         neg_uz = [sb("neg_uz%d" % t, [P, WINDOW], F32) for t in range(PACK)]
         for table in neg_y + neg_uz:
-            nc.gpsimd.memset(table[:, S:WINDOW], 0.0)
+            nc.vector.memset(table[:, S:WINDOW], 0.0)
 
         lists = {}
-        for name, src in (("offs", offs), ("pk", pk), ("dp1", dp1), ("dp2", dp2)):
+
+        def load_list(name, src):
             lists[name] = keep.tile([P, src.shape[1]], U16, name="list_" + name)
             nc.sync.dma_start(lists[name][:], src)
 
+        load_list("offs", offs)
+
         for q in range(4):
-            nc.scalar.dma_start(
+            nc.sync.dma_start(
                 out=x_scale_rows[32 * q : 32 * q + 4 * PASSES, :].bitcast(I32),
                 in_=x_scales[:, 4 * q : 4 * q + 4, :].bitcast(I32),
             )
@@ -67,6 +71,10 @@ def tile_picked_yresolv_dep_p_kernel(
                     out=raw[name, g][:],
                     in_=w[g * K_PASS : (g + 1) * K_PASS, :].rearrange("(p j) c -> p j c", j=PACK),
                 )
+            if name == "w1":
+                load_list("pk", pk)
+                load_list("dp1", dp1)
+                load_list("dp2", dp2)
         unit_raw = sb("unit_raw", [P, PACK, 8], F32)
         unit_by_tile = unit.rearrange("(a t i) o -> t a i o", t=PACK, i=4)
         with nc.allow_non_contiguous_dma(reason="one value a partition"):
@@ -124,8 +132,8 @@ def tile_picked_yresolv_dep_p_kernel(
 
         group("w1", 0, 0, 2, nc.scalar.copy)
         group("w1", 0, 2, 4, nc.vector.tensor_copy)
-        quantize("w1", 0, 0)
         quantize("w1", 0, 2)
+        quantize("w1", 0, 0)
         group("w1", 1, 0, 1, nc.vector.tensor_copy)
         group("w1", 1, 1, 3, nc.scalar.copy)
         group("w1", 1, 3, 4, nc.vector.tensor_copy)
@@ -138,58 +146,54 @@ def tile_picked_yresolv_dep_p_kernel(
         def offsets(name, c0, c1):
             return lists[name][:, c0 // LIST_ROWS : c1 // LIST_ROWS]
 
-        steps = [(b, t) for b in range(BLOCKS) for t in range(PACK)]
-        wide = {}
-        for b in range(BLOCKS):
-            for name in ("yp", "y1", "low", "cmp"):
-                for t in range(PACK):
-                    wide[name, b, t] = sb("%s_%d_%d" % (name, b, t), [P, BLOCK], F32)
-            wide["prod", b] = sb("prod_%d" % b, [P, PACK, BLOCK], F32)
+        made = {}
+        prod = [sb("prod_%d" % b, [P, PACK, BLOCK], F32) for b in range(BLOCKS)]
 
-        def fetch_y(s):
-            b, t = steps[s]
-            c0, c1 = b * BLOCK, (b + 1) * BLOCK
-            if b == 0:
-                nc.scalar.activation(neg_y[t][:, 0:S], acc["w1", t][:], COPY, scale=-1.0)
-            nc.scalar.activation(wide["yp", b, t][:], neg_y[t][:].indirect(offsets("pk", c0, c1)), COPY)
-            if s == 0:
-                nc.vector.tensor_copy(wide["y1", b, t][:], neg_y[t][:].indirect(offsets("dp1", c0, c1)))
+        def evacuate_y(t):
+            if t == 1:
+                nc.vector.tensor_scalar(neg_y[t][:, 0:S], acc["w1", t][:], -1.0, None, ALU.mult)
             else:
-                nc.scalar.activation(wide["y1", b, t][:], neg_y[t][:].indirect(offsets("dp1", c0, c1)), COPY)
-
-        def lower(s):
-            b, t = steps[s]
-            nc.vector.tensor_tensor(wide["low", b, t][:], wide["yp", b, t][:], wide["y1", b, t][:], ALU.max)
-
-        def add_y2(s):
-            b, t = steps[s]
-            window = neg_y[t][:].indirect(offsets("dp2", b * BLOCK, (b + 1) * BLOCK))
-            nc.vector.tensor_tensor(wide["cmp", b, t][:], window, wide["low", b, t][:], ALU.add)
-
-        def times_zp(s):
-            b, t = steps[s]
-            window = neg_uz[t][:].indirect(offsets("pk", b * BLOCK, (b + 1) * BLOCK))
-            nc.vector.tensor_tensor(wide["prod", b][:, t, :], window, wide["cmp", b, t][:], ALU.mult)
+                nc.scalar.activation(neg_y[t][:, 0:S], acc["w1", t][:], COPY, scale=-1.0)
 
         def evacuate_z(t):
-            nc.scalar.activation(neg_uz[t][:, 0:S], acc["w2", t][:], COPY, scale=neg_unit[:, t : t + 1])
+            if t == 0:
+                nc.vector.tensor_scalar(neg_uz[t][:, 0:S], acc["w2", t][:], neg_unit[:, t : t + 1], None, ALU.mult)
+            else:
+                nc.scalar.activation(neg_uz[t][:, 0:S], acc["w2", t][:], COPY, scale=neg_unit[:, t : t + 1])
 
-        zd2 = {}
+        def fetch_y(t, b):
+            for name in ("pk", "dp1"):
+                made[name, t, b] = sb("neg_y_%s_%d_%d" % (name, t, b), [P, BLOCK], F32, tag="neg_y_" + name, bufs=FETCH_BUFS)
+                window = neg_y[t][:].indirect(offsets(name, b * BLOCK, (b + 1) * BLOCK))
+                nc.scalar.activation(made[name, t, b][:], window, COPY)
+
+        def lower(t, b):
+            tag = "grp_w2_1_%d" % (2 * b) if t == 0 else "neg_cmp_%d_%d" % (t - 1, b)
+            made["low", t, b] = sb("neg_low_%d_%d" % (t, b), [P, BLOCK], F32, tag=tag)
+            nc.vector.tensor_tensor(made["low", t, b][:], made["pk", t, b][:], made["dp1", t, b][:], ALU.max)
+
+        def add_y2(t, b):
+            made["cmp", t, b] = sb("neg_cmp_%d_%d" % (t, b), [P, BLOCK], F32)
+            window = neg_y[t][:].indirect(offsets("dp2", b * BLOCK, (b + 1) * BLOCK))
+            nc.vector.tensor_tensor(made["cmp", t, b][:], window, made["low", t, b][:], ALU.add)
+
+        def times_zp(t, b):
+            window = neg_uz[t][:].indirect(offsets("pk", b * BLOCK, (b + 1) * BLOCK))
+            nc.vector.tensor_tensor(prod[b][:, t, :], window, made["cmp", t, b][:], ALU.mult)
+
         hid = {}
 
         def fetch_zd2(c0, c1, t):
-            if t == 0:
-                zd2[c0] = sb("zd2_%d" % c0, [P, PACK, c1 - c0], F32)
-            nc.scalar.activation(zd2[c0][:, t, :], neg_uz[t][:].indirect(offsets("dp2", c0, c1)), COPY)
+            start = PACK * c0 + t * (c1 - c0)
+            nc.scalar.activation(zd2[:, start : start + c1 - c0], neg_uz[t][:].indirect(offsets("dp2", c0, c1)), COPY)
 
         def finish_hid(c0, c1):
             b = c0 // BLOCK
             hid[c0] = sb("hid_%d" % c0, [P, PACK * (c1 - c0)], BF16)
-            prod = wide["prod", b][:, :, c0 - b * BLOCK : c1 - b * BLOCK]
             nc.vector.tensor_tensor(
                 hid[c0][:].rearrange("p (c i t) -> p c t i", i=4, t=PACK),
-                prod.rearrange("p t (c i) -> p c t i", i=4),
-                zd2[c0][:].rearrange("p t (c i) -> p c t i", i=4),
+                prod[b][:, :, c0 - b * BLOCK : c1 - b * BLOCK].rearrange("p t (c i) -> p c t i", i=4),
+                zd2[:, PACK * c0 : PACK * c1].rearrange("p (t c i) -> p c t i", t=PACK, i=4),
                 ALU.add,
             )
 
@@ -212,12 +216,12 @@ def tile_picked_yresolv_dep_p_kernel(
             nc.scalar.copy(result[:], sums[:])
             nc.sync.dma_start(out=out[:, c0:c1], in_=result[:])
 
-        fetch_y(0)
+        evacuate_y(0)
+        fetch_y(0, 0)
+        fetch_y(0, 1)
+        evacuate_y(1)
         group("w2", 0, 0, 4, nc.vector.tensor_copy)
-        lower(0)
         quantize("w2", 0, 0)
-        add_y2(0)
-        fetch_y(1)
         group("w2", 1, 0, 2, nc.vector.tensor_copy)
         group("w2", 1, 2, 4, nc.vector.tensor_copy)
         quantize("w2", 1, 0)
@@ -226,46 +230,33 @@ def tile_picked_yresolv_dep_p_kernel(
         quantize("w2", 1, 2)
         for t in range(PACK):
             project("w2", t)
-        lower(1)
         w3_grouped = sb("w3_grouped", [P, PACK * N], BF16)
-        nc.vector.tensor_copy(
-            w3_grouped[:].rearrange("p (c i t) -> p c t i", i=4, t=PACK),
-            w3_raw[:].rearrange("p t (c i) -> p c t i", i=4),
-        )
-        add_y2(1)
         w3_codes = sb("w3_codes", [P, N], U32)
         w3_scales = sb("w3_scales", [P, N], U8)
-        nc.vector.quantize_mx(out=w3_codes[:].bitcast(FP8X4), scales=w3_scales[:], in_=w3_grouped[:])
-
-        fetch_y(2)
-        evacuate_z(0)
-        evacuate_z(1)
-        lower(2)
-        times_zp(0)
-        add_y2(2)
-        fetch_y(3)
-        evacuate_z(2)
-        evacuate_z(3)
-        times_zp(1)
-        lower(3)
-        times_zp(2)
-        add_y2(3)
-        for s in range(PACK, 2 * PACK):
-            fetch_y(s)
-            if s < PACK + 2:
-                fetch_zd2(0, BLOCK, 2 * (s - PACK))
-                fetch_zd2(0, BLOCK, 2 * (s - PACK) + 1)
-            lower(s)
-            times_zp(s - 1)
-            add_y2(s)
-            if s == PACK + 1:
-                finish_hid(0, BLOCK)
-            if s == PACK + 2:
-                build(0, BLOCK, 0)
-        times_zp(2 * PACK - 1)
-        c0 = BLOCK
+        for t in range(PACK):
+            if t > 1:
+                evacuate_y(t)
+            if t > 0:
+                fetch_y(t, 0)
+                fetch_y(t, 1)
+            lower(t, 0)
+            lower(t, 1)
+            evacuate_z(t)
+            add_y2(t, 0)
+            add_y2(t, 1)
+            times_zp(t, 0)
+            times_zp(t, 1)
+            if t == 0:
+                nc.scalar.copy(
+                    w3_grouped[:].rearrange("p (c i t) -> p c t i", i=4, t=PACK),
+                    w3_raw[:].rearrange("p t (c i) -> p c t i", i=4),
+                )
+            if t == 1:
+                nc.vector.quantize_mx(out=w3_codes[:].bitcast(FP8X4), scales=w3_scales[:], in_=w3_grouped[:])
+        zd2 = sb("neg_uz_dp2", [P, PACK * U], F32, tag="neg_cmp_0_0")
+        c0 = 0
         pieces = []
-        for width in LAST_PIECES:
+        for width in PIECES:
             pieces.append((c0, c0 + width))
             c0 = c0 + width
         for c0, c1 in pieces:
@@ -274,5 +265,5 @@ def tile_picked_yresolv_dep_p_kernel(
         for n, (c0, c1) in enumerate(pieces):
             finish_hid(c0, c1)
             if n > 0:
-                build(pieces[n - 1][0], pieces[n - 1][1], n)
-        build(pieces[-1][0], pieces[-1][1], 0)
+                build(pieces[n - 1][0], pieces[n - 1][1], n - 1)
+        build(pieces[-1][0], pieces[-1][1], len(pieces) - 1)

from contextlib import ExitStack

import concourse.mybir as mybir

K, T, S, N, H, U = 1024, 1024, 512, 128, 512, 1024
FLOPS = 2 * (2 * K * H * S + H * N * U)

F32 = mybir.dt.float32
BF16 = mybir.dt.bfloat16
I32 = mybir.dt.int32
U32 = mybir.dt.uint32
U16 = mybir.dt.uint16
U8 = mybir.dt.uint8
FP8X4 = mybir.dt.float8_e4m3fn_x4
ALU = mybir.AluOpType
COPY = mybir.ActivationFunctionType.Copy

P = 128
PACK = 4
K_PASS = P * PACK
PASSES = K // K_PASS
LIST_ROWS = 16
BLOCK = 512
BLOCKS = U // BLOCK
WINDOW = S + LIST_ROWS
FETCH_BUFS = 4
PIECES = (512, 256, 128, 128)


def tile_picked_yresolv_dep_p_kernel(
    tc, x_words, x_scales, w1, w2, unit, w3, offs, pk, dp1, dp2, out
):
    nc = tc.nc
    with ExitStack() as ctx:
        keep = ctx.enter_context(tc.tile_pool(name="keep", bufs=1))
        psum = ctx.enter_context(tc.psum_pool(name="psum", bufs=1))

        def sb(name, shape, dtype, tag=None, bufs=1):
            return keep.tile(shape, dtype, name=name, tag=tag or name, bufs=bufs, align_bytes=64)

        x_scale_rows = sb("x_scale_rows", [P, T], U8)
        nc.gpsimd.memset(x_scale_rows[:].bitcast(I32), 0)
        neg_y = [sb("neg_y%d" % t, [P, WINDOW], F32) for t in range(PACK)]
        neg_uz = [sb("neg_uz%d" % t, [P, WINDOW], F32) for t in range(PACK)]
        for table in neg_y + neg_uz:
            nc.vector.memset(table[:, S:WINDOW], 0.0)

        lists = {}

        def load_list(name, src):
            lists[name] = keep.tile([P, src.shape[1]], U16, name="list_" + name)
            nc.sync.dma_start(lists[name][:], src)

        load_list("offs", offs)

        for q in range(4):
            nc.sync.dma_start(
                out=x_scale_rows[32 * q : 32 * q + 4 * PASSES, :].bitcast(I32),
                in_=x_scales[:, 4 * q : 4 * q + 4, :].bitcast(I32),
            )
        x_all = []
        for g in range(PASSES):
            words = sb("x_all%d" % g, [P, T], I32)
            nc.sync.dma_start(out=words[:], in_=x_words[g].rearrange("p n j -> p (n j)").bitcast(I32))
            x_all.append(words)
        raw = {}
        for name, w in (("w1", w1), ("w2", w2)):
            for g in range(PASSES):
                raw[name, g] = sb("raw_%s_%d" % (name, g), [P, PACK, H], F32)
                nc.sync.dma_start(
                    out=raw[name, g][:],
                    in_=w[g * K_PASS : (g + 1) * K_PASS, :].rearrange("(p j) c -> p j c", j=PACK),
                )
            if name == "w1":
                load_list("pk", pk)
                load_list("dp1", dp1)
                load_list("dp2", dp2)
        unit_raw = sb("unit_raw", [P, PACK, 8], F32)
        unit_by_tile = unit.rearrange("(a t i) o -> t a i o", t=PACK, i=4)
        with nc.allow_non_contiguous_dma(reason="one value a partition"):
            for t in range(PACK):
                nc.sync.dma_start(out=unit_raw[:, t, 0:1], in_=unit_by_tile[t])
        w3_raw = sb("w3_raw", [P, PACK, N], F32)
        w3_by_tile = w3.rearrange("(a t i) n -> t a i n", t=PACK, i=4)
        for t in range(PACK):
            nc.sync.dma_start(out=w3_raw[:, t, :], in_=w3_by_tile[t])

        x_picked = []
        for g in range(PASSES):
            picked = sb("x_picked%d" % g, [P, S], U32)
            nc.vector.tensor_copy(picked[:], x_all[g][:].bitcast(U32).indirect(lists["offs"][:]))
            x_picked.append(picked)
        x_picked_scales = sb("x_picked_scales", [P, S], U8)
        nc.vector.tensor_copy(x_picked_scales[:], x_scale_rows[:].indirect(lists["offs"][:]))

        grouped = {}
        lhs = {}

        def group(name, g, t0, t1, copy):
            tile = sb("grp_%s_%d_%d" % (name, g, t0), [P, (t1 - t0) * K_PASS], BF16)
            copy(
                tile[:].rearrange("p (t a i j) -> p t a j i", a=32, i=4, j=PACK),
                raw[name, g][:].rearrange("p j (a t i) -> p t a j i", t=PACK, i=4)[:, t0:t1],
            )
            grouped[name, g, t0] = (tile, t1)

        def quantize(name, g, t0):
            tile, t1 = grouped[name, g, t0]
            width = (t1 - t0) * P
            codes = sb("codes_%s_%d_%d" % (name, g, t0), [P, width], U32)
            scales = sb("scales_%s_%d_%d" % (name, g, t0), [P, width], U8)
            nc.vector.quantize_mx(out=codes[:].bitcast(FP8X4), scales=scales[:], in_=tile[:])
            for t in range(t0, t1):
                cols = slice((t - t0) * P, (t - t0 + 1) * P)
                lhs[name, g, t] = (codes[:, cols], scales[:, cols])

        acc = {}

        def project(name, t):
            acc[name, t] = psum.tile([P, S], F32, name="acc_%s_%d" % (name, t), tag="bank_%s_%d" % (name, t))
            for g in range(PASSES):
                codes, scales = lhs[name, g, t]
                nc.tensor.matmul_mx(
                    out=acc[name, t][:],
                    lhsT=codes.bitcast(FP8X4),
                    lhsT_scale=scales,
                    rhs=x_picked[g][:].bitcast(FP8X4),
                    rhs_scale=x_picked_scales[4 * g : P, :],
                    start=(g == 0),
                    stop=(g == PASSES - 1),
                )

        group("w1", 0, 0, 2, nc.scalar.copy)
        group("w1", 0, 2, 4, nc.vector.tensor_copy)
        quantize("w1", 0, 2)
        quantize("w1", 0, 0)
        group("w1", 1, 0, 1, nc.vector.tensor_copy)
        group("w1", 1, 1, 3, nc.scalar.copy)
        group("w1", 1, 3, 4, nc.vector.tensor_copy)
        quantize("w1", 1, 0)
        quantize("w1", 1, 3)
        quantize("w1", 1, 1)
        for t in range(PACK):
            project("w1", t)

        def offsets(name, c0, c1):
            return lists[name][:, c0 // LIST_ROWS : c1 // LIST_ROWS]

        made = {}
        prod = [sb("prod_%d" % b, [P, PACK, BLOCK], F32) for b in range(BLOCKS)]

        def evacuate_y(t):
            if t == 1:
                nc.vector.tensor_scalar(neg_y[t][:, 0:S], acc["w1", t][:], -1.0, None, ALU.mult)
            else:
                nc.scalar.activation(neg_y[t][:, 0:S], acc["w1", t][:], COPY, scale=-1.0)

        def evacuate_z(t):
            if t == 0:
                nc.vector.tensor_scalar(neg_uz[t][:, 0:S], acc["w2", t][:], neg_unit[:, t : t + 1], None, ALU.mult)
            else:
                nc.scalar.activation(neg_uz[t][:, 0:S], acc["w2", t][:], COPY, scale=neg_unit[:, t : t + 1])

        def fetch_y(t, b):
            for name in ("pk", "dp1"):
                made[name, t, b] = sb("neg_y_%s_%d_%d" % (name, t, b), [P, BLOCK], F32, tag="neg_y_" + name, bufs=FETCH_BUFS)
                window = neg_y[t][:].indirect(offsets(name, b * BLOCK, (b + 1) * BLOCK))
                nc.scalar.activation(made[name, t, b][:], window, COPY)

        def lower(t, b):
            tag = "grp_w2_1_%d" % (2 * b) if t == 0 else "neg_cmp_%d_%d" % (t - 1, b)
            made["low", t, b] = sb("neg_low_%d_%d" % (t, b), [P, BLOCK], F32, tag=tag)
            nc.vector.tensor_tensor(made["low", t, b][:], made["pk", t, b][:], made["dp1", t, b][:], ALU.max)

        def add_y2(t, b):
            made["cmp", t, b] = sb("neg_cmp_%d_%d" % (t, b), [P, BLOCK], F32)
            window = neg_y[t][:].indirect(offsets("dp2", b * BLOCK, (b + 1) * BLOCK))
            nc.vector.tensor_tensor(made["cmp", t, b][:], window, made["low", t, b][:], ALU.add)

        def times_zp(t, b):
            window = neg_uz[t][:].indirect(offsets("pk", b * BLOCK, (b + 1) * BLOCK))
            nc.vector.tensor_tensor(prod[b][:, t, :], window, made["cmp", t, b][:], ALU.mult)

        hid = {}

        def fetch_zd2(c0, c1, t):
            start = PACK * c0 + t * (c1 - c0)
            nc.scalar.activation(zd2[:, start : start + c1 - c0], neg_uz[t][:].indirect(offsets("dp2", c0, c1)), COPY)

        def finish_hid(c0, c1):
            b = c0 // BLOCK
            hid[c0] = sb("hid_%d" % c0, [P, PACK * (c1 - c0)], BF16)
            nc.vector.tensor_tensor(
                hid[c0][:].rearrange("p (c i t) -> p c t i", i=4, t=PACK),
                prod[b][:, :, c0 - b * BLOCK : c1 - b * BLOCK].rearrange("p t (c i) -> p c t i", i=4),
                zd2[:, PACK * c0 : PACK * c1].rearrange("p (t c i) -> p c t i", t=PACK, i=4),
                ALU.add,
            )

        def build(c0, c1, bank):
            width = c1 - c0
            codes = sb("hid_codes_%d" % c0, [P, width], U32)
            scales = sb("hid_scales_%d" % c0, [P, width], U8)
            nc.vector.quantize_mx(out=codes[:].bitcast(FP8X4), scales=scales[:], in_=hid[c0][:])
            sums = psum.tile([P, width], F32, name="sums_%d" % c0, tag="bank_w1_%d" % bank)
            nc.tensor.matmul_mx(
                out=sums[:],
                lhsT=w3_codes[:].bitcast(FP8X4),
                lhsT_scale=w3_scales[:],
                rhs=codes[:].bitcast(FP8X4),
                rhs_scale=scales[:],
                start=True,
                stop=True,
            )
            result = sb("result_%d" % c0, [P, width], F32)
            nc.scalar.copy(result[:], sums[:])
            nc.sync.dma_start(out=out[:, c0:c1], in_=result[:])

        evacuate_y(0)
        fetch_y(0, 0)
        fetch_y(0, 1)
        evacuate_y(1)
        group("w2", 0, 0, 4, nc.vector.tensor_copy)
        quantize("w2", 0, 0)
        group("w2", 1, 0, 2, nc.vector.tensor_copy)
        group("w2", 1, 2, 4, nc.vector.tensor_copy)
        quantize("w2", 1, 0)
        neg_unit = sb("neg_unit", [P, PACK], F32)
        nc.vector.tensor_scalar(neg_unit[:], unit_raw[:, :, 0], -1.0, None, ALU.mult)
        quantize("w2", 1, 2)
        for t in range(PACK):
            project("w2", t)
        w3_grouped = sb("w3_grouped", [P, PACK * N], BF16)
        w3_codes = sb("w3_codes", [P, N], U32)
        w3_scales = sb("w3_scales", [P, N], U8)
        for t in range(PACK):
            if t > 1:
                evacuate_y(t)
            if t > 0:
                fetch_y(t, 0)
                fetch_y(t, 1)
            lower(t, 0)
            lower(t, 1)
            evacuate_z(t)
            add_y2(t, 0)
            add_y2(t, 1)
            times_zp(t, 0)
            times_zp(t, 1)
            if t == 0:
                nc.scalar.copy(
                    w3_grouped[:].rearrange("p (c i t) -> p c t i", i=4, t=PACK),
                    w3_raw[:].rearrange("p t (c i) -> p c t i", i=4),
                )
            if t == 1:
                nc.vector.quantize_mx(out=w3_codes[:].bitcast(FP8X4), scales=w3_scales[:], in_=w3_grouped[:])
        zd2 = sb("neg_uz_dp2", [P, PACK * U], F32, tag="neg_cmp_0_0")
        c0 = 0
        pieces = []
        for width in PIECES:
            pieces.append((c0, c0 + width))
            c0 = c0 + width
        for c0, c1 in pieces:
            for t in range(PACK):
                fetch_zd2(c0, c1, t)
        for n, (c0, c1) in enumerate(pieces):
            finish_hid(c0, c1)
            if n > 0:
                build(pieces[n - 1][0], pieces[n - 1][1], n - 1)
        build(pieces[-1][0], pieces[-1][1], len(pieces) - 1)
